import numpy as np
import ml_dtypes


def mxq(x, axis, fmt="e4m3"):
    dtype, down = {"e4m3": (ml_dtypes.float8_e4m3fn, 7), "e5m2": (ml_dtypes.float8_e5m2, 14)}[fmt]
    v = np.moveaxis(np.asarray(x, np.float32).astype(ml_dtypes.bfloat16).astype(np.float64), axis, -1)
    blocks = v.reshape(v.shape[:-1] + (-1, 32))
    amax = np.abs(blocks).max(-1, keepdims=True)
    byte = np.maximum(np.where(amax > 0, np.frexp(amax)[1] - 1 + 127, 0) - down, 1)
    scale = np.exp2(byte - 127.0)
    codes = (blocks / scale).astype(np.float32).astype(dtype).astype(np.float64)
    return np.moveaxis((codes * scale).reshape(v.shape), -1, axis)


WIDE = False


def mx_kscale(k):
    if not WIDE:
        return np.ones(k)
    levels = np.array([10, -10, 5, -5, 0])
    if k % 512:
        return np.exp2(np.random.permutation(np.resize(levels, k // 32))).repeat(32)
    a = np.empty((k // 512, 16))
    for p in range(k // 512):
        a[p, :8] = np.random.permutation(np.resize(levels, 8))
        for g in range(8):
            far = levels[np.abs(levels - a[p, g]) >= 10]
            a[p, g + 8] = far[np.random.randint(len(far))]
    return np.exp2(a.ravel()).repeat(32)


def f64(x):
    return np.asarray(x).astype(np.float64)


def striped(idx):
    return np.tile(idx.reshape(-1, 16).T, (8, 1)).astype(np.uint16)


def unstriped(offs):
    return offs[:16].T.reshape(-1).astype(np.int64)


def pack_weight(w):
    k, n = w.shape
    w = f64(np.asarray(w, np.float32).astype(ml_dtypes.bfloat16)).reshape(k // 32, 32, n)
    amax = np.abs(w).max(1)
    byte = np.clip(np.where(amax > 0, np.frexp(amax)[1] - 1 + 127 - 7, 1), 1, 254)
    scaled = (w * np.exp2(127.0 - byte)[:, None, :]).reshape(k, n).astype(np.float32)
    words = np.ascontiguousarray(scaled.reshape(k // 512, 128, 4, n).transpose(0, 1, 3, 2)).astype(ml_dtypes.float8_e4m3fn).view(np.uint8)
    return words, np.ascontiguousarray(byte.astype(np.uint8).reshape(k // 512, 16, n))


def unpack_weight(words, scales):
    g, p, n, _ = words.shape
    vals = np.ascontiguousarray(words).view(ml_dtypes.float8_e4m3fn).astype(np.float64) * np.repeat(np.exp2(scales.astype(np.float64) - 127.0), 8, axis=1)[..., None]
    return vals.transpose(0, 1, 3, 2).reshape(g * 512, n)


def relu(v):
    return np.maximum(v, 0.0)


K, T, S, H, G, R = 1024, 2048, 512, 512, 2048, 512


def setup_inputs():
    n = np.random.standard_normal
    s = mx_kscale(K)[:, None]
    u = mx_kscale(H)
    packed_xT = pack_weight(n((K, T)) * s)
    packed_vT = pack_weight(n((H, G)) / np.sqrt(H) / u[:, None])
    return {
        "x_words": packed_xT[0],
        "x_scales": packed_xT[1],
        "w1": (n((K, H)) / np.sqrt(K) / s * u).astype(np.float32),
        "v_words": packed_vT[0],
        "v_scales": packed_vT[1],
        "offs": striped(np.random.permutation(T)[:S]),
        "cand": striped(np.random.permutation(G)[:R]),
    }


def reference(x_words, x_scales, w1, v_words, v_scales, offs, cand):
    v_cand = unpack_weight(v_words, v_scales)[:, unstriped(cand)]
    xq = unpack_weight(x_words, x_scales)[:, unstriped(offs)]
    h = mxq(f64(w1), 0, "e4m3").T @ xq
    y = v_cand.T @ mxq(h, 0, "e4m3")
    lg = 1.5 * (np.log(relu(y) + 0.05))
    top = lg.reshape(len(lg), -1, 4).max(axis=2)
    ex = np.exp(lg - np.repeat(top, 4, axis=1))
    total = ex.reshape(len(ex), -1, 4).sum(axis=2)
    a = ex / np.repeat(total, 4, axis=1)
    asc = a * y
    sc = asc.reshape(len(asc), -1, 4).sum(axis=2)
    ex = np.exp(sc - sc.max(axis=1, keepdims=True))
    return ex / ex.sum(axis=1, keepdims=True)

@@ -1,0 +1,242 @@
+from contextlib import ExitStack
+
+import concourse.mybir as mybir
+from concourse.masks import make_identity
+
+K, T, S, H, G, R = 1024, 2048, 512, 512, 2048, 512
+FLOPS = 2 * K * H * S + 2 * H * R * S
+
+F32 = mybir.dt.float32
+BF16 = mybir.dt.bfloat16
+I32 = mybir.dt.int32
+U32 = mybir.dt.uint32
+U16 = mybir.dt.uint16
+U8 = mybir.dt.uint8
+FP8X4 = mybir.dt.float8_e4m3fn_x4
+ALU = mybir.AluOpType
+ACT = mybir.ActivationFunctionType
+AX = mybir.AxisListType
+
+P = 128
+PACK = 4
+PASSES = K // (P * PACK)
+D = 4
+USERS = S // D
+CHUNKS = S // P
+CU = P // D
+TT = R // P
+FLOOR = 0.05
+EXP_MASK = 0x7F800000
+SHRINK = 1.0 / 32.0
+TINY = 1e-30
+V_ROW = 8
+
+
+def tile_picked_ylabel_soft_p_kernel(
+    tc, x_words, x_scales, w1, v_words, v_scales, offs, cand, out
+):
+    nc = tc.nc
+    with ExitStack() as ctx:
+        keep = ctx.enter_context(tc.tile_pool(name="keep", bufs=1))
+        work = ctx.enter_context(tc.tile_pool(name="work", bufs=4))
+        psum = ctx.enter_context(tc.psum_pool(name="psum", bufs=1))
+
+        offs_sb = keep.tile([P, S // 16], U16, name="offs_sb")
+        cand_sb = keep.tile([P, R // 16], U16, name="cand_sb")
+        xs_table = keep.tile([P, T], U8, name="xs_table", align_bytes=64)
+        vs_table = keep.tile([P, G], U8, name="vs_table", align_bytes=64)
+        x_table = [keep.tile([P, T], U32, name="x_table%d" % g, align_bytes=64) for g in range(PASSES)]
+        v_table = keep.tile([P, G], U32, name="v_table", align_bytes=64)
+        w_raw = [keep.tile([P, PACK, H], F32, name="w_raw%d" % g) for g in range(PASSES)]
+        ident = keep.tile([P, P], F32, name="ident")
+        one = keep.tile([P, 1], F32, name="one")
+        warm = keep.tile([P, 1], F32, name="warm")
+
+        nc.gpsimd.memset(xs_table[:].bitcast(I32), 0)
+        nc.gpsimd.memset(vs_table[:].bitcast(I32), 0)
+        nc.vector.memset(one[:], 1.0)
+        nc.scalar.activation(out=warm[:], in_=one[:], func=ACT.Abs_reciprocal_sqrt)
+        make_identity(nc, ident[:])
+
+        def load_w(g):
+            rows = w1[g * P * PACK : (g + 1) * P * PACK, :]
+            nc.sync.dma_start(out=w_raw[g][:], in_=rows.rearrange("(p j) c -> p j c", j=PACK))
+
+        def load_words(table, words):
+            nc.sync.dma_start(out=table[:].bitcast(I32), in_=words.rearrange("p n t -> p (n t)").bitcast(I32))
+
+        load_w(0)
+        nc.sync.dma_start(offs_sb[:], offs)
+        for q in range(4):
+            nc.sync.dma_start(
+                out=xs_table[32 * q : 32 * q + 4 * PASSES, :].bitcast(I32),
+                in_=x_scales[:, 4 * q : 4 * q + 4, :].bitcast(I32),
+            )
+        nc.sync.dma_start(cand_sb[:], cand)
+        load_w(1)
+        for q in range(4):
+            nc.sync.dma_start(
+                out=vs_table[32 * q + V_ROW : 32 * q + V_ROW + 4, :].bitcast(I32),
+                in_=v_scales[0, 4 * q : 4 * q + 4, :].bitcast(I32),
+            )
+        for g in range(PASSES):
+            load_words(x_table[g], x_words[g])
+        load_words(v_table, v_words[0])
+
+        xs = keep.tile([P, S], U8, name="xs", align_bytes=64)
+        vs = keep.tile([P, R], U8, name="vs", align_bytes=64)
+        xq = [keep.tile([P, S], U32, name="xq%d" % g, align_bytes=64) for g in range(PASSES)]
+        vq = keep.tile([P, R], U32, name="vq", align_bytes=64)
+        wq = [keep.tile([P, H], U32, name="wq%d" % g, align_bytes=64) for g in range(PASSES)]
+        ws = [keep.tile([P, H], U8, name="ws%d" % g, align_bytes=64) for g in range(PASSES)]
+
+        nc.vector.tensor_copy(xs[:], xs_table[:].indirect(offs_sb[:]))
+        nc.vector.tensor_copy(vs[:], vs_table[:].indirect(cand_sb[:]))
+
+        for g in range(PASSES):
+            w_bf = keep.tile([P, H * PACK], BF16, name="w_bf%d" % g, align_bytes=64)
+            nc.scalar.copy(
+                out=w_bf[:].rearrange("p (t m j) -> p m j t", t=PACK, j=PACK),
+                in_=w_raw[g][:].rearrange("p j (m t) -> p m j t", t=PACK),
+            )
+            nc.vector.quantize_mx(out=wq[g][:].bitcast(FP8X4), scales=ws[g][:], in_=w_bf[:])
+
+        def gather_halves(picked, table, offsets):
+            for half in range(2):
+                nc.vector.tensor_copy(
+                    picked[:, half * 256 : (half + 1) * 256],
+                    table[:].indirect(offsets[:, half * 16 : (half + 1) * 16]),
+                )
+
+        nc.vector.tensor_copy(xq[0][:], x_table[0][:].indirect(offs_sb[:]))
+        gather_halves(xq[1], x_table[1], offs_sb)
+
+        neg_sc = psum.tile([P, CHUNKS, P], F32, name="neg_sc")
+        hq, hs, y, ratio, weight, weighted = {}, {}, {}, {}, {}, {}
+
+        def hidden(b):
+            cols = slice(b * P, (b + 1) * P)
+            h = psum.tile([P, PACK, P], F32, name="h", tag="acc", bufs=7)
+            for t in range(PACK):
+                tcols = slice(t * P, (t + 1) * P)
+                for g in range(PASSES):
+                    nc.tensor.matmul_mx(
+                        out=h[:, t, :],
+                        lhsT=wq[g][:, tcols].bitcast(FP8X4),
+                        lhsT_scale=ws[g][:, tcols],
+                        rhs=xq[g][:, cols].bitcast(FP8X4),
+                        rhs_scale=xs[4 * g : P, cols],
+                        start=(g == 0),
+                        stop=(g == PASSES - 1),
+                    )
+            h_bf = work.tile([P, P * PACK], BF16, name="h_bf", align_bytes=64, bufs=4)
+            nc.scalar.copy(
+                out=h_bf[:].rearrange("p (d v t) -> p d v t", d=D, t=PACK),
+                in_=h[:].rearrange("p t (v d) -> p d v t", d=D),
+            )
+            hq[b] = work.tile([P, P], U32, name="hq", align_bytes=64, bufs=4)
+            hs[b] = work.tile([P, P], U8, name="hs", align_bytes=64, bufs=4)
+            nc.vector.quantize_mx(out=hq[b][:].bitcast(FP8X4), scales=hs[b][:], in_=h_bf[:])
+
+        def planes(bank):
+            return bank[:].rearrange("p tt (d v) -> p d tt v", d=D)
+
+        def as_planes(tile):
+            return tile[:].rearrange("p d (tt v) -> p d tt v", tt=TT)
+
+        def scores(b):
+            y[b] = psum.tile([P, TT, P], F32, name="y", tag="acc", bufs=7)
+            for tt in range(TT):
+                tcols = slice(tt * P, (tt + 1) * P)
+                nc.tensor.matmul_mx(
+                    out=y[b][:, tt, :],
+                    lhsT=vq[:, tcols].bitcast(FP8X4),
+                    lhsT_scale=vs[V_ROW:P, tcols],
+                    rhs=hq[b][:].bitcast(FP8X4),
+                    rhs_scale=hs[b][:],
+                    start=True,
+                    stop=True,
+                )
+            pos = work.tile([P, D, P], F32, name="pos")
+            nc.scalar.activation(out=as_planes(pos), in_=planes(y[b]), func=ACT.Relu)
+            pair_max = work.tile([P, 2, P], F32, name="pair_max")
+            nc.vector.tensor_tensor(out=pair_max[:], in0=pos[:, 0:2, :], in1=pos[:, 2:4, :], op=ALU.max)
+            top = work.tile([P, P], F32, name="top")
+            nc.vector.scalar_tensor_tensor(
+                out=top[:], in0=pair_max[:, 0, :], scalar=FLOOR, in1=pair_max[:, 1, :], op0=ALU.max, op1=ALU.max
+            )
+            inv_top = work.tile([P, P], I32, name="inv_top")
+            nc.vector.tensor_scalar(
+                out=inv_top[:], in0=top[:].bitcast(I32), scalar1=EXP_MASK, scalar2=EXP_MASK,
+                op0=ALU.bitwise_and, op1=ALU.bitwise_xor,
+            )
+            ratio[b] = work.tile([P, D, P], F32, name="ratio")
+            nc.vector.scalar_tensor_tensor(
+                out=ratio[b][:], in0=pos[:], scalar=FLOOR,
+                in1=inv_top[:].bitcast(F32).unsqueeze(1).to_broadcast([P, D, P]),
+                op0=ALU.add, op1=ALU.mult,
+            )
+
+        def weights(b):
+            inv_root = work.tile([P, D, P], F32, name="inv_root")
+            nc.scalar.activation(
+                out=inv_root[:], in_=ratio[b][:], func=ACT.Abs_reciprocal_sqrt, scale=SHRINK, bias=TINY
+            )
+            squared = work.tile([P, D, P], F32, name="squared")
+            nc.scalar.activation(out=squared[:], in_=ratio[b][:], func=ACT.Square, scale=SHRINK)
+            weight[b] = work.tile([P, D, P], F32, name="weight")
+            nc.vector.tensor_tensor(out=weight[b][:], in0=squared[:], in1=inv_root[:], op=ALU.mult)
+            weighted[b] = work.tile([P, D, P], F32, name="weighted")
+            nc.vector.tensor_tensor(out=as_planes(weighted[b]), in0=planes(y[b]), in1=as_planes(weight[b]), op=ALU.mult)
+
+        def sum_planes(bank, tile):
+            for d in range(D):
+                nc.tensor.matmul(
+                    bank[:], lhsT=tile[:, d, :], rhs=ident[:], start=(d == 0), stop=(d == D - 1), is_transpose=True
+                )
+
+        def mix(b):
+            total = psum.tile([P, P], F32, name="total", tag="acc", bufs=7)
+            sum_planes(total, weight[b])
+            inv_root_total = work.tile([P, P], F32, name="inv_root_total")
+            nc.scalar.activation(out=inv_root_total[:], in_=total[:], func=ACT.Abs_reciprocal_sqrt)
+            inv_total = work.tile([P, P], F32, name="inv_total")
+            nc.scalar.activation(out=inv_total[:], in_=inv_root_total[:], func=ACT.Square)
+            mixed = psum.tile([P, P], F32, name="mixed", tag="acc", bufs=7)
+            sum_planes(mixed, weighted[b])
+            neg_sc_t = work.tile([P, P], F32, name="neg_sc_t")
+            nc.vector.scalar_tensor_tensor(
+                out=neg_sc_t[:], in0=mixed[:], scalar=-1.0, in1=inv_total[:], op0=ALU.mult, op1=ALU.mult
+            )
+            nc.tensor.transpose(neg_sc[:, b, :], neg_sc_t[:], ident[:])
+
+        hidden(0)
+        gather_halves(vq, v_table, cand_sb)
+        hidden(1)
+        scores(0)
+        hidden(2)
+        scores(1)
+        hidden(3)
+        scores(2)
+        weights(0)
+        scores(3)
+        for b in range(CHUNKS):
+            if b + 1 < CHUNKS:
+                weights(b + 1)
+            mix(b)
+
+        by_tile = neg_sc[:].rearrange("p b (tt v) -> p tt b v", tt=TT)
+        neg_max = keep.tile([P, TT], F32, name="neg_max")
+        nc.vector.tensor_reduce(out=neg_max[:], in_=by_tile, axis=AX.XY, op=ALU.min)
+        for tt in range(TT):
+            ex = work.tile([P, USERS], F32, name="ex", bufs=TT)
+            row_sum = work.tile([P, 1], F32, name="row_sum", bufs=TT)
+            nc.scalar.activation(
+                out=ex[:].rearrange("p (b v) -> p b v", b=CHUNKS), in_=by_tile[:, tt, :, :], func=ACT.Exp,
+                scale=-1.0, bias=neg_max[:, tt : tt + 1], accum_out=row_sum[:],
+            )
+            inv_sum = work.tile([P, 1], F32, name="inv_sum", bufs=TT)
+            nc.vector.reciprocal(out=inv_sum[:], in_=row_sum[:])
+            prob = work.tile([P, USERS], F32, name="prob", bufs=TT)
+            nc.vector.tensor_scalar(out=prob[:], in0=ex[:], scalar1=inv_sum[:], scalar2=None, op0=ALU.mult)
+            nc.sync.dma_start(out=out[tt * P : (tt + 1) * P, :], in_=prob[:])

@@ -26,7 +26,7 @@ CHUNKS = S // P
 CU = P // D
 TT = R // P
 FLOOR = 0.05
-EXP_MASK = 0x7F800000
+FLOOR_BITS = float(0x3D4CCCCD)
 SHRINK = 1.0 / 32.0
 TINY = 1e-30
 V_ROW = 8
@@ -56,7 +56,6 @@ def tile_picked_ylabel_soft_p_kernel(
         nc.gpsimd.memset(vs_table[:].bitcast(I32), 0)
         nc.vector.memset(one[:], 1.0)
         nc.scalar.activation(out=warm[:], in_=one[:], func=ACT.Abs_reciprocal_sqrt)
-        make_identity(nc, ident[:])
 
         def load_w(g):
             rows = w1[g * P * PACK : (g + 1) * P * PACK, :]
@@ -65,23 +64,30 @@ def tile_picked_ylabel_soft_p_kernel(
         def load_words(table, words):
             nc.sync.dma_start(out=table[:].bitcast(I32), in_=words.rearrange("p n t -> p (n t)").bitcast(I32))
 
+        def load_scales(table, row, scales, q):
+            nc.sync.dma_start(
+                out=table[32 * q + row : 32 * q + row + 4, :].bitcast(I32),
+                in_=scales[4 * q : 4 * q + 4, :].bitcast(I32),
+            )
+
+        small = [lambda: nc.sync.dma_start(offs_sb[:], offs)]
+        small += [
+            (lambda g=g, q=q: load_scales(xs_table, 4 * g, x_scales[g], q)) for g in range(PASSES) for q in range(4)
+        ]
+        small += [lambda: nc.sync.dma_start(cand_sb[:], cand)]
+        small += [(lambda q=q: load_scales(vs_table, V_ROW, v_scales[0], q)) for q in range(4)]
         load_w(0)
-        nc.sync.dma_start(offs_sb[:], offs)
-        for q in range(4):
-            nc.sync.dma_start(
-                out=xs_table[32 * q : 32 * q + 4 * PASSES, :].bitcast(I32),
-                in_=x_scales[:, 4 * q : 4 * q + 4, :].bitcast(I32),
-            )
-        nc.sync.dma_start(cand_sb[:], cand)
+        for load in small[0:6]:
+            load()
         load_w(1)
-        for q in range(4):
-            nc.sync.dma_start(
-                out=vs_table[32 * q + V_ROW : 32 * q + V_ROW + 4, :].bitcast(I32),
-                in_=v_scales[0, 4 * q : 4 * q + 4, :].bitcast(I32),
-            )
+        for load in small[6:10]:
+            load()
         for g in range(PASSES):
             load_words(x_table[g], x_words[g])
+        for load in small[10:]:
+            load()
         load_words(v_table, v_words[0])
+        make_identity(nc, ident[:])
 
         xs = keep.tile([P, S], U8, name="xs", align_bytes=64)
         vs = keep.tile([P, R], U8, name="vs", align_bytes=64)
@@ -90,16 +96,17 @@ def tile_picked_ylabel_soft_p_kernel(
         wq = [keep.tile([P, H], U32, name="wq%d" % g, align_bytes=64) for g in range(PASSES)]
         ws = [keep.tile([P, H], U8, name="ws%d" % g, align_bytes=64) for g in range(PASSES)]
 
-        nc.vector.tensor_copy(xs[:], xs_table[:].indirect(offs_sb[:]))
-        nc.vector.tensor_copy(vs[:], vs_table[:].indirect(cand_sb[:]))
-
         for g in range(PASSES):
-            w_bf = keep.tile([P, H * PACK], BF16, name="w_bf%d" % g, align_bytes=64)
-            nc.scalar.copy(
-                out=w_bf[:].rearrange("p (t m j) -> p m j t", t=PACK, j=PACK),
-                in_=w_raw[g][:].rearrange("p j (m t) -> p m j t", t=PACK),
-            )
-            nc.vector.quantize_mx(out=wq[g][:].bitcast(FP8X4), scales=ws[g][:], in_=w_bf[:])
+            for half, copy in enumerate((nc.vector.tensor_copy, nc.scalar.copy)):
+                w_bf = keep.tile([P, H * PACK // 2], BF16, name="w_bf%d%d" % (g, half), align_bytes=64)
+                copy(
+                    out=w_bf[:].rearrange("p (t m j) -> p m j t", t=2, j=PACK),
+                    in_=w_raw[g][:].rearrange("p j (m t) -> p m j t", t=PACK)[:, :, :, 2 * half : 2 * half + 2],
+                )
+                cols = slice(half * H // 2, (half + 1) * H // 2)
+                nc.vector.quantize_mx(out=wq[g][:, cols].bitcast(FP8X4), scales=ws[g][:, cols], in_=w_bf[:])
+
+        nc.vector.tensor_copy(xs[:], xs_table[:].indirect(offs_sb[:]))
 
         def gather_halves(picked, table, offsets):
             for half in range(2):
@@ -110,13 +117,14 @@ def tile_picked_ylabel_soft_p_kernel(
 
         nc.vector.tensor_copy(xq[0][:], x_table[0][:].indirect(offs_sb[:]))
         gather_halves(xq[1], x_table[1], offs_sb)
+        nc.vector.tensor_copy(vs[:], vs_table[:].indirect(cand_sb[:]))
 
         neg_sc = psum.tile([P, CHUNKS, P], F32, name="neg_sc")
-        hq, hs, y, ratio, weight, weighted = {}, {}, {}, {}, {}, {}
+        hq, hs, y, ratio, weight, inv_total = {}, {}, {}, {}, {}, {}
 
         def hidden(b):
             cols = slice(b * P, (b + 1) * P)
-            h = psum.tile([P, PACK, P], F32, name="h", tag="acc", bufs=7)
+            h = psum.tile([P, PACK, P], F32, name="h", tag="short", bufs=2)
             for t in range(PACK):
                 tcols = slice(t * P, (t + 1) * P)
                 for g in range(PASSES):
@@ -145,7 +153,7 @@ def tile_picked_ylabel_soft_p_kernel(
             return tile[:].rearrange("p d (tt v) -> p d tt v", tt=TT)
 
         def scores(b):
-            y[b] = psum.tile([P, TT, P], F32, name="y", tag="acc", bufs=7)
+            y[b] = psum.tile([P, TT, P], F32, name="y", tag="long", bufs=4)
             for tt in range(TT):
                 tcols = slice(tt * P, (tt + 1) * P)
                 nc.tensor.matmul_mx(
@@ -157,18 +165,17 @@ def tile_picked_ylabel_soft_p_kernel(
                     start=True,
                     stop=True,
                 )
+            top = work.tile([P, P], F32, name="top")
+            nc.vector.tensor_reduce(
+                out=top[:].rearrange("p (tt v) -> p tt v", tt=TT),
+                in_=y[b][:].rearrange("p tt (d v) -> p tt v d", d=D), axis=AX.X, op=ALU.max,
+            )
             pos = work.tile([P, D, P], F32, name="pos")
             nc.scalar.activation(out=as_planes(pos), in_=planes(y[b]), func=ACT.Relu)
-            pair_max = work.tile([P, 2, P], F32, name="pair_max")
-            nc.vector.tensor_tensor(out=pair_max[:], in0=pos[:, 0:2, :], in1=pos[:, 2:4, :], op=ALU.max)
-            top = work.tile([P, P], F32, name="top")
-            nc.vector.scalar_tensor_tensor(
-                out=top[:], in0=pair_max[:, 0, :], scalar=FLOOR, in1=pair_max[:, 1, :], op0=ALU.max, op1=ALU.max
-            )
             inv_top = work.tile([P, P], I32, name="inv_top")
             nc.vector.tensor_scalar(
-                out=inv_top[:], in0=top[:].bitcast(I32), scalar1=EXP_MASK, scalar2=EXP_MASK,
-                op0=ALU.bitwise_and, op1=ALU.bitwise_xor,
+                out=inv_top[:], in0=top[:].bitcast(I32), scalar1=FLOOR_BITS, scalar2=-1.0,
+                op0=ALU.max, op1=ALU.mult,
             )
             ratio[b] = work.tile([P, D, P], F32, name="ratio")
             nc.vector.scalar_tensor_tensor(
@@ -180,14 +187,18 @@ def tile_picked_ylabel_soft_p_kernel(
         def weights(b):
             inv_root = work.tile([P, D, P], F32, name="inv_root")
             nc.scalar.activation(
-                out=inv_root[:], in_=ratio[b][:], func=ACT.Abs_reciprocal_sqrt, scale=SHRINK, bias=TINY
+                out=inv_root[:], in_=ratio[b][:], func=ACT.Abs_reciprocal_sqrt, scale=-SHRINK, bias=TINY
             )
             squared = work.tile([P, D, P], F32, name="squared")
             nc.scalar.activation(out=squared[:], in_=ratio[b][:], func=ACT.Square, scale=SHRINK)
             weight[b] = work.tile([P, D, P], F32, name="weight")
             nc.vector.tensor_tensor(out=weight[b][:], in0=squared[:], in1=inv_root[:], op=ALU.mult)
-            weighted[b] = work.tile([P, D, P], F32, name="weighted")
-            nc.vector.tensor_tensor(out=as_planes(weighted[b]), in0=planes(y[b]), in1=as_planes(weight[b]), op=ALU.mult)
+            total = psum.tile([P, P], F32, name="total", tag="short", bufs=2)
+            sum_planes(total, weight[b])
+            inv_root_total = work.tile([P, P], F32, name="inv_root_total")
+            nc.scalar.activation(out=inv_root_total[:], in_=total[:], func=ACT.Abs_reciprocal_sqrt)
+            inv_total[b] = work.tile([P, P], F32, name="inv_total")
+            nc.scalar.activation(out=inv_total[b][:], in_=inv_root_total[:], func=ACT.Square)
 
         def sum_planes(bank, tile):
             for d in range(D):
@@ -196,33 +207,25 @@ def tile_picked_ylabel_soft_p_kernel(
                 )
 
         def mix(b):
-            total = psum.tile([P, P], F32, name="total", tag="acc", bufs=7)
-            sum_planes(total, weight[b])
-            inv_root_total = work.tile([P, P], F32, name="inv_root_total")
-            nc.scalar.activation(out=inv_root_total[:], in_=total[:], func=ACT.Abs_reciprocal_sqrt)
-            inv_total = work.tile([P, P], F32, name="inv_total")
-            nc.scalar.activation(out=inv_total[:], in_=inv_root_total[:], func=ACT.Square)
-            mixed = psum.tile([P, P], F32, name="mixed", tag="acc", bufs=7)
-            sum_planes(mixed, weighted[b])
+            weighted = work.tile([P, D, P], F32, name="weighted")
+            nc.vector.tensor_tensor(out=as_planes(weighted), in0=planes(y[b]), in1=as_planes(weight[b]), op=ALU.mult)
+            mixed = psum.tile([P, P], F32, name="mixed", tag="long", bufs=4)
+            sum_planes(mixed, weighted)
             neg_sc_t = work.tile([P, P], F32, name="neg_sc_t")
             nc.vector.scalar_tensor_tensor(
-                out=neg_sc_t[:], in0=mixed[:], scalar=-1.0, in1=inv_total[:], op0=ALU.mult, op1=ALU.mult
+                out=neg_sc_t[:], in0=mixed[:], scalar=-1.0, in1=inv_total[b][:], op0=ALU.mult, op1=ALU.mult
             )
             nc.tensor.transpose(neg_sc[:, b, :], neg_sc_t[:], ident[:])
 
         hidden(0)
         gather_halves(vq, v_table, cand_sb)
-        hidden(1)
-        scores(0)
-        hidden(2)
-        scores(1)
-        hidden(3)
-        scores(2)
-        weights(0)
-        scores(3)
         for b in range(CHUNKS):
             if b + 1 < CHUNKS:
-                weights(b + 1)
+                hidden(b + 1)
+            scores(b)
+        for b in range(CHUNKS):
+            weights(b)
+        for b in range(CHUNKS):
             mix(b)
 
         by_tile = neg_sc[:].rearrange("p b (tt v) -> p tt b v", tt=TT)

@@ -19,17 +19,18 @@ AX = mybir.AxisListType
 
 P = 128
 PACK = 4
+QUADRANTS = 4
 PASSES = K // (P * PACK)
 D = 4
 USERS = S // D
-CHUNKS = S // P
-CU = P // D
-TT = R // P
+RUNS = 4
 FLOOR = 0.05
 FLOOR_BITS = float(0x3D4CCCCD)
 SHRINK = 1.0 / 32.0
 TINY = 1e-30
 V_ROW = 8
+IN_FLIGHT = 8
+WARM_PASSES = 6
 
 
 def tile_picked_ylabel_soft_p_kernel(
@@ -46,16 +47,16 @@ def tile_picked_ylabel_soft_p_kernel(
         xs_table = keep.tile([P, T], U8, name="xs_table", align_bytes=64)
         vs_table = keep.tile([P, G], U8, name="vs_table", align_bytes=64)
         x_table = [keep.tile([P, T], U32, name="x_table%d" % g, align_bytes=64) for g in range(PASSES)]
-        v_table = keep.tile([P, G], U32, name="v_table", align_bytes=64)
+        v_table = keep.tile([P, G], U32, name="v_table", tag="v_words", align_bytes=64)
         w_raw = [keep.tile([P, PACK, H], F32, name="w_raw%d" % g) for g in range(PASSES)]
         ident = keep.tile([P, P], F32, name="ident")
-        one = keep.tile([P, 1], F32, name="one")
-        warm = keep.tile([P, 1], F32, name="warm")
+        shrink_in = keep.tile([P, 1], F32, name="shrink_in")
+        shrink = keep.tile([P, 1], F32, name="shrink")
 
         nc.gpsimd.memset(xs_table[:].bitcast(I32), 0)
         nc.gpsimd.memset(vs_table[:].bitcast(I32), 0)
-        nc.vector.memset(one[:], 1.0)
-        nc.scalar.activation(out=warm[:], in_=one[:], func=ACT.Abs_reciprocal_sqrt)
+        nc.vector.memset(shrink_in[:], 1.0 / SHRINK**2)
+        nc.scalar.activation(out=shrink[:], in_=shrink_in[:], func=ACT.Abs_reciprocal_sqrt)
 
         def load_w(g):
             rows = w1[g * P * PACK : (g + 1) * P * PACK, :]
@@ -70,22 +71,20 @@ def tile_picked_ylabel_soft_p_kernel(
                 in_=scales[4 * q : 4 * q + 4, :].bitcast(I32),
             )
 
-        small = [lambda: nc.sync.dma_start(offs_sb[:], offs)]
-        small += [
-            (lambda g=g, q=q: load_scales(xs_table, 4 * g, x_scales[g], q)) for g in range(PASSES) for q in range(4)
-        ]
-        small += [lambda: nc.sync.dma_start(cand_sb[:], cand)]
-        small += [(lambda q=q: load_scales(vs_table, V_ROW, v_scales[0], q)) for q in range(4)]
+        x_scale_rows = [(g, q) for g in range(PASSES) for q in range(QUADRANTS)]
+        early = IN_FLIGHT - PASSES - 1
         load_w(0)
-        for load in small[0:6]:
-            load()
+        nc.sync.dma_start(offs_sb[:], offs)
+        for g, q in x_scale_rows[:early]:
+            load_scales(xs_table, 4 * g, x_scales[g], q)
         load_w(1)
-        for load in small[6:10]:
-            load()
+        for g, q in x_scale_rows[early:]:
+            load_scales(xs_table, 4 * g, x_scales[g], q)
+        nc.sync.dma_start(cand_sb[:], cand)
         for g in range(PASSES):
             load_words(x_table[g], x_words[g])
-        for load in small[10:]:
-            load()
+        for q in range(QUADRANTS):
+            load_scales(vs_table, V_ROW, v_scales[0], q)
         load_words(v_table, v_words[0])
         make_identity(nc, ident[:])
 
@@ -103,143 +102,183 @@ def tile_picked_ylabel_soft_p_kernel(
                     out=w_bf[:].rearrange("p (t m j) -> p m j t", t=2, j=PACK),
                     in_=w_raw[g][:].rearrange("p j (m t) -> p m j t", t=PACK)[:, :, :, 2 * half : 2 * half + 2],
                 )
-                cols = slice(half * H // 2, (half + 1) * H // 2)
-                nc.vector.quantize_mx(out=wq[g][:, cols].bitcast(FP8X4), scales=ws[g][:, cols], in_=w_bf[:])
+                places = slice(half * H // 2, (half + 1) * H // 2)
+                nc.vector.quantize_mx(out=wq[g][:, places].bitcast(FP8X4), scales=ws[g][:, places], in_=w_bf[:])
 
         nc.vector.tensor_copy(xs[:], xs_table[:].indirect(offs_sb[:]))
-
-        def gather_halves(picked, table, offsets):
+        for g in range(PASSES):
             for half in range(2):
                 nc.vector.tensor_copy(
-                    picked[:, half * 256 : (half + 1) * 256],
-                    table[:].indirect(offsets[:, half * 16 : (half + 1) * 16]),
+                    xq[g][:, half * S // 2 : (half + 1) * S // 2],
+                    x_table[g][:].indirect(offs_sb[:, half * S // 32 : (half + 1) * S // 32]),
                 )
-
-        nc.vector.tensor_copy(xq[0][:], x_table[0][:].indirect(offs_sb[:]))
-        gather_halves(xq[1], x_table[1], offs_sb)
         nc.vector.tensor_copy(vs[:], vs_table[:].indirect(cand_sb[:]))
 
-        neg_sc = psum.tile([P, CHUNKS, P], F32, name="neg_sc")
-        hq, hs, y, ratio, weight, inv_total = {}, {}, {}, {}, {}, {}
+        neg_sc = [psum.tile([P, 2, P], F32, name="neg_sc%d" % a) for a in range(2)]
+        hs = [keep.tile([P, 2 * P], U8, name="hs%d" % c, align_bytes=64) for c in range(2)]
+        by_columns = [(a, c) for c in range(2) for a in range(2)]
+        by_rows = [(a, c) for a in range(2) for c in range(2)]
+        y = {chunk: psum.tile([P, RUNS, P], F32, name="y", tag="long", bufs=4) for chunk in by_rows}
+        ratio, weight, inv_total = {}, {}, {}
 
         def hidden(b):
-            cols = slice(b * P, (b + 1) * P)
+            entries = slice(b * P, (b + 1) * P)
             h = psum.tile([P, PACK, P], F32, name="h", tag="short", bufs=2)
             for t in range(PACK):
-                tcols = slice(t * P, (t + 1) * P)
+                places = slice(t * P, (t + 1) * P)
                 for g in range(PASSES):
                     nc.tensor.matmul_mx(
                         out=h[:, t, :],
-                        lhsT=wq[g][:, tcols].bitcast(FP8X4),
-                        lhsT_scale=ws[g][:, tcols],
-                        rhs=xq[g][:, cols].bitcast(FP8X4),
-                        rhs_scale=xs[4 * g : P, cols],
+                        lhsT=wq[g][:, places].bitcast(FP8X4),
+                        lhsT_scale=ws[g][:, places],
+                        rhs=xq[g][:, entries].bitcast(FP8X4),
+                        rhs_scale=xs[4 * g : P, entries],
                         start=(g == 0),
                         stop=(g == PASSES - 1),
                     )
-            h_bf = work.tile([P, P * PACK], BF16, name="h_bf", align_bytes=64, bufs=4)
+            h_bf = work.tile([P, P * PACK], BF16, name="h_bf", align_bytes=64)
             nc.scalar.copy(
                 out=h_bf[:].rearrange("p (d v t) -> p d v t", d=D, t=PACK),
                 in_=h[:].rearrange("p t (v d) -> p d v t", d=D),
             )
-            hq[b] = work.tile([P, P], U32, name="hq", align_bytes=64, bufs=4)
-            hs[b] = work.tile([P, P], U8, name="hs", align_bytes=64, bufs=4)
-            nc.vector.quantize_mx(out=hq[b][:].bitcast(FP8X4), scales=hs[b][:], in_=h_bf[:])
+            part = slice((b % 2) * P, (b % 2 + 1) * P)
+            nc.vector.quantize_mx(out=hq[b // 2][:, part].bitcast(FP8X4), scales=hs[b // 2][:, part], in_=h_bf[:])
 
-        def planes(bank):
-            return bank[:].rearrange("p tt (d v) -> p d tt v", d=D)
+        def bank_by_interest(bank):
+            return bank[:].rearrange("p run (d v) -> p d run v", d=D)
 
-        def as_planes(tile):
-            return tile[:].rearrange("p d (tt v) -> p d tt v", tt=TT)
+        def tile_by_interest(tile):
+            return tile[:].rearrange("p d (run v) -> p d run v", run=RUNS)
 
-        def scores(b):
-            y[b] = psum.tile([P, TT, P], F32, name="y", tag="long", bufs=4)
-            for tt in range(TT):
-                tcols = slice(tt * P, (tt + 1) * P)
+        def scores(chunk):
+            a, c = chunk
+            for l in range(2):
+                rows = slice((2 * a + l) * P, (2 * a + l + 1) * P)
                 nc.tensor.matmul_mx(
-                    out=y[b][:, tt, :],
-                    lhsT=vq[:, tcols].bitcast(FP8X4),
-                    lhsT_scale=vs[V_ROW:P, tcols],
-                    rhs=hq[b][:].bitcast(FP8X4),
-                    rhs_scale=hs[b][:],
+                    out=y[chunk][:, 2 * l : 2 * l + 2, :].rearrange("p u n -> p (u n)"),
+                    lhsT=vq[:, rows].bitcast(FP8X4),
+                    lhsT_scale=vs[V_ROW:P, rows],
+                    rhs=hq[c].bitcast(FP8X4),
+                    rhs_scale=hs[c][:],
                     start=True,
                     stop=True,
                 )
             top = work.tile([P, P], F32, name="top")
             nc.vector.tensor_reduce(
-                out=top[:].rearrange("p (tt v) -> p tt v", tt=TT),
-                in_=y[b][:].rearrange("p tt (d v) -> p tt v d", d=D), axis=AX.X, op=ALU.max,
+                out=top[:].rearrange("p (run v) -> p run v", run=RUNS),
+                in_=y[chunk][:].rearrange("p run (d v) -> p run v d", d=D),
+                axis=AX.X,
+                op=ALU.max,
             )
             pos = work.tile([P, D, P], F32, name="pos")
-            nc.scalar.activation(out=as_planes(pos), in_=planes(y[b]), func=ACT.Relu)
-            inv_top = work.tile([P, P], I32, name="inv_top")
+            nc.scalar.activation(out=tile_by_interest(pos), in_=bank_by_interest(y[chunk]), func=ACT.Relu)
+            neg_inv_top = work.tile([P, P], I32, name="neg_inv_top")
             nc.vector.tensor_scalar(
-                out=inv_top[:], in0=top[:].bitcast(I32), scalar1=FLOOR_BITS, scalar2=-1.0,
-                op0=ALU.max, op1=ALU.mult,
+                out=neg_inv_top[:],
+                in0=top[:].bitcast(I32),
+                scalar1=FLOOR_BITS,
+                scalar2=-1.0,
+                op0=ALU.max,
+                op1=ALU.mult,
             )
-            ratio[b] = work.tile([P, D, P], F32, name="ratio")
+            ratio[chunk] = work.tile([P, D, P], F32, name="ratio")
             nc.vector.scalar_tensor_tensor(
-                out=ratio[b][:], in0=pos[:], scalar=FLOOR,
-                in1=inv_top[:].bitcast(F32).unsqueeze(1).to_broadcast([P, D, P]),
-                op0=ALU.add, op1=ALU.mult,
+                out=ratio[chunk][:],
+                in0=pos[:],
+                scalar=FLOOR,
+                in1=neg_inv_top[:].bitcast(F32).unsqueeze(1).to_broadcast([P, D, P]),
+                op0=ALU.add,
+                op1=ALU.mult,
             )
 
-        def weights(b):
+        def weights(chunk):
             inv_root = work.tile([P, D, P], F32, name="inv_root")
             nc.scalar.activation(
-                out=inv_root[:], in_=ratio[b][:], func=ACT.Abs_reciprocal_sqrt, scale=-SHRINK, bias=TINY
+                out=inv_root[:], in_=ratio[chunk][:], func=ACT.Abs_reciprocal_sqrt, scale=-SHRINK, bias=TINY
             )
             squared = work.tile([P, D, P], F32, name="squared")
-            nc.scalar.activation(out=squared[:], in_=ratio[b][:], func=ACT.Square, scale=SHRINK)
-            weight[b] = work.tile([P, D, P], F32, name="weight")
-            nc.vector.tensor_tensor(out=weight[b][:], in0=squared[:], in1=inv_root[:], op=ALU.mult)
-            total = psum.tile([P, P], F32, name="total", tag="short", bufs=2)
-            sum_planes(total, weight[b])
-            inv_root_total = work.tile([P, P], F32, name="inv_root_total")
-            nc.scalar.activation(out=inv_root_total[:], in_=total[:], func=ACT.Abs_reciprocal_sqrt)
-            inv_total[b] = work.tile([P, P], F32, name="inv_total")
-            nc.scalar.activation(out=inv_total[b][:], in_=inv_root_total[:], func=ACT.Square)
+            nc.scalar.activation(out=squared[:], in_=ratio[chunk][:], func=ACT.Square, scale=shrink[:])
+            weight[chunk] = work.tile([P, D, P], F32, name="weight")
+            nc.vector.tensor_tensor(out=weight[chunk][:], in0=squared[:], in1=inv_root[:], op=ALU.mult)
 
-        def sum_planes(bank, tile):
+        def sum_interests(bank, tile):
             for d in range(D):
                 nc.tensor.matmul(
                     bank[:], lhsT=tile[:, d, :], rhs=ident[:], start=(d == 0), stop=(d == D - 1), is_transpose=True
                 )
 
-        def mix(b):
+        def totals(chunk):
+            total = psum.tile([P, P], F32, name="total", tag="short", bufs=2)
+            sum_interests(total, weight[chunk])
+            inv_root_total = work.tile([P, P], F32, name="inv_root_total")
+            nc.scalar.activation(out=inv_root_total[:], in_=total[:], func=ACT.Abs_reciprocal_sqrt)
+            inv_total[chunk] = work.tile([P, P], F32, name="inv_total")
+            nc.scalar.activation(out=inv_total[chunk][:], in_=inv_root_total[:], func=ACT.Square)
+
+        def mix(chunk):
+            a, c = chunk
             weighted = work.tile([P, D, P], F32, name="weighted")
-            nc.vector.tensor_tensor(out=as_planes(weighted), in0=planes(y[b]), in1=as_planes(weight[b]), op=ALU.mult)
+            nc.vector.tensor_tensor(
+                out=tile_by_interest(weighted),
+                in0=bank_by_interest(y[chunk]),
+                in1=tile_by_interest(weight[chunk]),
+                op=ALU.mult,
+            )
             mixed = psum.tile([P, P], F32, name="mixed", tag="long", bufs=4)
-            sum_planes(mixed, weighted)
-            neg_sc_t = work.tile([P, P], F32, name="neg_sc_t")
+            sum_interests(mixed, weighted)
+            neg_sc_turned = work.tile([P, P], F32, name="neg_sc_turned")
             nc.vector.scalar_tensor_tensor(
-                out=neg_sc_t[:], in0=mixed[:], scalar=-1.0, in1=inv_total[b][:], op0=ALU.mult, op1=ALU.mult
+                out=neg_sc_turned[:], in0=mixed[:], scalar=-1.0, in1=inv_total[chunk][:], op0=ALU.mult, op1=ALU.mult
             )
-            nc.tensor.transpose(neg_sc[:, b, :], neg_sc_t[:], ident[:])
+            nc.tensor.transpose(neg_sc[a][:, c, :], neg_sc_turned[:], ident[:])
 
-        hidden(0)
-        gather_halves(vq, v_table, cand_sb)
-        for b in range(CHUNKS):
-            if b + 1 < CHUNKS:
-                hidden(b + 1)
-            scores(b)
-        for b in range(CHUNKS):
-            weights(b)
-        for b in range(CHUNKS):
-            mix(b)
+        def finish(a):
+            by_row_tile = neg_sc[a][:].rearrange("p c (l user) -> p l c user", l=2)
+            neg_max = work.tile([P, 2], F32, name="neg_max")
+            nc.vector.tensor_reduce(out=neg_max[:], in_=by_row_tile, axis=AX.XY, op=ALU.min)
+            for l in range(2):
+                ex = work.tile([P, USERS], F32, name="ex")
+                row_sum = work.tile([P, 1], F32, name="row_sum")
+                nc.scalar.activation(
+                    out=ex[:].rearrange("p (c user) -> p c user", c=2),
+                    in_=by_row_tile[:, l, :, :],
+                    func=ACT.Exp,
+                    scale=-1.0,
+                    bias=neg_max[:, l : l + 1],
+                    accum_out=row_sum[:],
+                )
+                inv_sum = work.tile([P, 1], F32, name="inv_sum")
+                nc.vector.reciprocal(out=inv_sum[:], in_=row_sum[:])
+                prob = work.tile([P, USERS], F32, name="prob")
+                nc.vector.tensor_scalar(out=prob[:], in0=ex[:], scalar1=inv_sum[:], scalar2=None, op0=ALU.mult)
+                nc.sync.dma_start(out=out[(2 * a + l) * P : (2 * a + l + 1) * P, :], in_=prob[:])
 
-        by_tile = neg_sc[:].rearrange("p b (tt v) -> p tt b v", tt=TT)
-        neg_max = keep.tile([P, TT], F32, name="neg_max")
-        nc.vector.tensor_reduce(out=neg_max[:], in_=by_tile, axis=AX.XY, op=ALU.min)
-        for tt in range(TT):
-            ex = work.tile([P, USERS], F32, name="ex", bufs=TT)
-            row_sum = work.tile([P, 1], F32, name="row_sum", bufs=TT)
-            nc.scalar.activation(
-                out=ex[:].rearrange("p (b v) -> p b v", b=CHUNKS), in_=by_tile[:, tt, :, :], func=ACT.Exp,
-                scale=-1.0, bias=neg_max[:, tt : tt + 1], accum_out=row_sum[:],
+        for n in range(WARM_PASSES):
+            places = slice(n % PACK * P, (n % PACK + 1) * P)
+            nc.tensor.matmul_mx(
+                out=y[by_rows[-1]][:, 0:2, :].rearrange("p u n -> p (u n)"),
+                lhsT=wq[0][:, places].bitcast(FP8X4),
+                lhsT_scale=ws[0][:, places],
+                rhs=xq[0][:, 0 : S // 2].bitcast(FP8X4),
+                rhs_scale=xs[:, 0 : S // 2],
+                start=True,
+                stop=True,
             )
-            inv_sum = work.tile([P, 1], F32, name="inv_sum", bufs=TT)
-            nc.vector.reciprocal(out=inv_sum[:], in_=row_sum[:])
-            prob = work.tile([P, USERS], F32, name="prob", bufs=TT)
-            nc.vector.tensor_scalar(out=prob[:], in0=ex[:], scalar1=inv_sum[:], scalar2=None, op0=ALU.mult)
-            nc.sync.dma_start(out=out[tt * P : (tt + 1) * P, :], in_=prob[:])
+
+        nc.vector.tensor_copy(vq[:], v_table[:].indirect(cand_sb[:]))
+        hq_all = keep.tile([P, S], U32, name="hq_all", tag="v_words", align_bytes=64)
+        hq = [hq_all[:, c * 2 * P : (c + 1) * 2 * P] for c in range(2)]
+
+        for b in range(S // P - 1):
+            hidden(b)
+        scores(by_columns[0])
+        hidden(S // P - 1)
+        for chunk in by_columns[1:]:
+            scores(chunk)
+        for stage in (weights, totals):
+            for chunk in by_columns:
+                stage(chunk)
+        for chunk in by_rows:
+            mix(chunk)
+        for a in range(2):
+            finish(a)

from contextlib import ExitStack

import concourse.mybir as mybir
from concourse.masks import make_identity

K, T, S, H, G, R = 1024, 2048, 512, 512, 2048, 512
FLOPS = 2 * K * H * S + 2 * H * R * S

F32 = mybir.dt.float32
BF16 = mybir.dt.bfloat16
I32 = mybir.dt.int32
U32 = mybir.dt.uint32
U16 = mybir.dt.uint16
U8 = mybir.dt.uint8
FP8X4 = mybir.dt.float8_e4m3fn_x4
ALU = mybir.AluOpType
ACT = mybir.ActivationFunctionType
AX = mybir.AxisListType

P = 128
PACK = 4
QUADRANTS = 4
PASSES = K // (P * PACK)
D = 4
USERS = S // D
RUNS = 4
FLOOR = 0.05
FLOOR_BITS = float(0x3D4CCCCD)
SHRINK = 1.0 / 32.0
TINY = 1e-30
V_ROW = 8
IN_FLIGHT = 8
WARM_PASSES = 6


def tile_picked_ylabel_soft_p_kernel(
    tc, x_words, x_scales, w1, v_words, v_scales, offs, cand, out
):
    nc = tc.nc
    with ExitStack() as ctx:
        keep = ctx.enter_context(tc.tile_pool(name="keep", bufs=1))
        work = ctx.enter_context(tc.tile_pool(name="work", bufs=4))
        psum = ctx.enter_context(tc.psum_pool(name="psum", bufs=1))

        offs_sb = keep.tile([P, S // 16], U16, name="offs_sb")
        cand_sb = keep.tile([P, R // 16], U16, name="cand_sb")
        xs_table = keep.tile([P, T], U8, name="xs_table", align_bytes=64)
        vs_table = keep.tile([P, G], U8, name="vs_table", align_bytes=64)
        x_table = [keep.tile([P, T], U32, name="x_table%d" % g, align_bytes=64) for g in range(PASSES)]
        v_table = keep.tile([P, G], U32, name="v_table", tag="v_words", align_bytes=64)
        w_raw = [keep.tile([P, PACK, H], F32, name="w_raw%d" % g) for g in range(PASSES)]
        ident = keep.tile([P, P], F32, name="ident")
        shrink_in = keep.tile([P, 1], F32, name="shrink_in")
        shrink = keep.tile([P, 1], F32, name="shrink")

        nc.gpsimd.memset(xs_table[:].bitcast(I32), 0)
        nc.gpsimd.memset(vs_table[:].bitcast(I32), 0)
        nc.vector.memset(shrink_in[:], 1.0 / SHRINK**2)
        nc.scalar.activation(out=shrink[:], in_=shrink_in[:], func=ACT.Abs_reciprocal_sqrt)

        def load_w(g):
            rows = w1[g * P * PACK : (g + 1) * P * PACK, :]
            nc.sync.dma_start(out=w_raw[g][:], in_=rows.rearrange("(p j) c -> p j c", j=PACK))

        def load_words(table, words):
            nc.sync.dma_start(out=table[:].bitcast(I32), in_=words.rearrange("p n t -> p (n t)").bitcast(I32))

        def load_scales(table, row, scales, q):
            nc.sync.dma_start(
                out=table[32 * q + row : 32 * q + row + 4, :].bitcast(I32),
                in_=scales[4 * q : 4 * q + 4, :].bitcast(I32),
            )

        x_scale_rows = [(g, q) for g in range(PASSES) for q in range(QUADRANTS)]
        early = IN_FLIGHT - PASSES - 1
        load_w(0)
        nc.sync.dma_start(offs_sb[:], offs)
        for g, q in x_scale_rows[:early]:
            load_scales(xs_table, 4 * g, x_scales[g], q)
        load_w(1)
        for g, q in x_scale_rows[early:]:
            load_scales(xs_table, 4 * g, x_scales[g], q)
        nc.sync.dma_start(cand_sb[:], cand)
        for g in range(PASSES):
            load_words(x_table[g], x_words[g])
        for q in range(QUADRANTS):
            load_scales(vs_table, V_ROW, v_scales[0], q)
        load_words(v_table, v_words[0])
        make_identity(nc, ident[:])

        xs = keep.tile([P, S], U8, name="xs", align_bytes=64)
        vs = keep.tile([P, R], U8, name="vs", align_bytes=64)
        xq = [keep.tile([P, S], U32, name="xq%d" % g, align_bytes=64) for g in range(PASSES)]
        vq = keep.tile([P, R], U32, name="vq", align_bytes=64)
        wq = [keep.tile([P, H], U32, name="wq%d" % g, align_bytes=64) for g in range(PASSES)]
        ws = [keep.tile([P, H], U8, name="ws%d" % g, align_bytes=64) for g in range(PASSES)]

        for g in range(PASSES):
            for half, copy in enumerate((nc.vector.tensor_copy, nc.scalar.copy)):
                w_bf = keep.tile([P, H * PACK // 2], BF16, name="w_bf%d%d" % (g, half), align_bytes=64)
                copy(
                    out=w_bf[:].rearrange("p (t m j) -> p m j t", t=2, j=PACK),
                    in_=w_raw[g][:].rearrange("p j (m t) -> p m j t", t=PACK)[:, :, :, 2 * half : 2 * half + 2],
                )
                places = slice(half * H // 2, (half + 1) * H // 2)
                nc.vector.quantize_mx(out=wq[g][:, places].bitcast(FP8X4), scales=ws[g][:, places], in_=w_bf[:])

        nc.vector.tensor_copy(xs[:], xs_table[:].indirect(offs_sb[:]))
        for g in range(PASSES):
            for half in range(2):
                nc.vector.tensor_copy(
                    xq[g][:, half * S // 2 : (half + 1) * S // 2],
                    x_table[g][:].indirect(offs_sb[:, half * S // 32 : (half + 1) * S // 32]),
                )
        nc.vector.tensor_copy(vs[:], vs_table[:].indirect(cand_sb[:]))

        neg_sc = [psum.tile([P, 2, P], F32, name="neg_sc%d" % a) for a in range(2)]
        hs = [keep.tile([P, 2 * P], U8, name="hs%d" % c, align_bytes=64) for c in range(2)]
        by_columns = [(a, c) for c in range(2) for a in range(2)]
        by_rows = [(a, c) for a in range(2) for c in range(2)]
        y = {chunk: psum.tile([P, RUNS, P], F32, name="y", tag="long", bufs=4) for chunk in by_rows}
        ratio, weight, inv_total = {}, {}, {}

        def hidden(b):
            entries = slice(b * P, (b + 1) * P)
            h = psum.tile([P, PACK, P], F32, name="h", tag="short", bufs=2)
            for t in range(PACK):
                places = slice(t * P, (t + 1) * P)
                for g in range(PASSES):
                    nc.tensor.matmul_mx(
                        out=h[:, t, :],
                        lhsT=wq[g][:, places].bitcast(FP8X4),
                        lhsT_scale=ws[g][:, places],
                        rhs=xq[g][:, entries].bitcast(FP8X4),
                        rhs_scale=xs[4 * g : P, entries],
                        start=(g == 0),
                        stop=(g == PASSES - 1),
                    )
            h_bf = work.tile([P, P * PACK], BF16, name="h_bf", align_bytes=64)
            nc.scalar.copy(
                out=h_bf[:].rearrange("p (d v t) -> p d v t", d=D, t=PACK),
                in_=h[:].rearrange("p t (v d) -> p d v t", d=D),
            )
            part = slice((b % 2) * P, (b % 2 + 1) * P)
            nc.vector.quantize_mx(out=hq[b // 2][:, part].bitcast(FP8X4), scales=hs[b // 2][:, part], in_=h_bf[:])

        def bank_by_interest(bank):
            return bank[:].rearrange("p run (d v) -> p d run v", d=D)

        def tile_by_interest(tile):
            return tile[:].rearrange("p d (run v) -> p d run v", run=RUNS)

        def scores(chunk):
            a, c = chunk
            for l in range(2):
                rows = slice((2 * a + l) * P, (2 * a + l + 1) * P)
                nc.tensor.matmul_mx(
                    out=y[chunk][:, 2 * l : 2 * l + 2, :].rearrange("p u n -> p (u n)"),
                    lhsT=vq[:, rows].bitcast(FP8X4),
                    lhsT_scale=vs[V_ROW:P, rows],
                    rhs=hq[c].bitcast(FP8X4),
                    rhs_scale=hs[c][:],
                    start=True,
                    stop=True,
                )
            top = work.tile([P, P], F32, name="top")
            nc.vector.tensor_reduce(
                out=top[:].rearrange("p (run v) -> p run v", run=RUNS),
                in_=y[chunk][:].rearrange("p run (d v) -> p run v d", d=D),
                axis=AX.X,
                op=ALU.max,
            )
            pos = work.tile([P, D, P], F32, name="pos")
            nc.scalar.activation(out=tile_by_interest(pos), in_=bank_by_interest(y[chunk]), func=ACT.Relu)
            neg_inv_top = work.tile([P, P], I32, name="neg_inv_top")
            nc.vector.tensor_scalar(
                out=neg_inv_top[:],
                in0=top[:].bitcast(I32),
                scalar1=FLOOR_BITS,
                scalar2=-1.0,
                op0=ALU.max,
                op1=ALU.mult,
            )
            ratio[chunk] = work.tile([P, D, P], F32, name="ratio")
            nc.vector.scalar_tensor_tensor(
                out=ratio[chunk][:],
                in0=pos[:],
                scalar=FLOOR,
                in1=neg_inv_top[:].bitcast(F32).unsqueeze(1).to_broadcast([P, D, P]),
                op0=ALU.add,
                op1=ALU.mult,
            )

        def weights(chunk):
            inv_root = work.tile([P, D, P], F32, name="inv_root")
            nc.scalar.activation(
                out=inv_root[:], in_=ratio[chunk][:], func=ACT.Abs_reciprocal_sqrt, scale=-SHRINK, bias=TINY
            )
            squared = work.tile([P, D, P], F32, name="squared")
            nc.scalar.activation(out=squared[:], in_=ratio[chunk][:], func=ACT.Square, scale=shrink[:])
            weight[chunk] = work.tile([P, D, P], F32, name="weight")
            nc.vector.tensor_tensor(out=weight[chunk][:], in0=squared[:], in1=inv_root[:], op=ALU.mult)

        def sum_interests(bank, tile):
            for d in range(D):
                nc.tensor.matmul(
                    bank[:], lhsT=tile[:, d, :], rhs=ident[:], start=(d == 0), stop=(d == D - 1), is_transpose=True
                )

        def totals(chunk):
            total = psum.tile([P, P], F32, name="total", tag="short", bufs=2)
            sum_interests(total, weight[chunk])
            inv_root_total = work.tile([P, P], F32, name="inv_root_total")
            nc.scalar.activation(out=inv_root_total[:], in_=total[:], func=ACT.Abs_reciprocal_sqrt)
            inv_total[chunk] = work.tile([P, P], F32, name="inv_total")
            nc.scalar.activation(out=inv_total[chunk][:], in_=inv_root_total[:], func=ACT.Square)

        def mix(chunk):
            a, c = chunk
            weighted = work.tile([P, D, P], F32, name="weighted")
            nc.vector.tensor_tensor(
                out=tile_by_interest(weighted),
                in0=bank_by_interest(y[chunk]),
                in1=tile_by_interest(weight[chunk]),
                op=ALU.mult,
            )
            mixed = psum.tile([P, P], F32, name="mixed", tag="long", bufs=4)
            sum_interests(mixed, weighted)
            neg_sc_turned = work.tile([P, P], F32, name="neg_sc_turned")
            nc.vector.scalar_tensor_tensor(
                out=neg_sc_turned[:], in0=mixed[:], scalar=-1.0, in1=inv_total[chunk][:], op0=ALU.mult, op1=ALU.mult
            )
            nc.tensor.transpose(neg_sc[a][:, c, :], neg_sc_turned[:], ident[:])

        def finish(a):
            by_row_tile = neg_sc[a][:].rearrange("p c (l user) -> p l c user", l=2)
            neg_max = work.tile([P, 2], F32, name="neg_max")
            nc.vector.tensor_reduce(out=neg_max[:], in_=by_row_tile, axis=AX.XY, op=ALU.min)
            for l in range(2):
                ex = work.tile([P, USERS], F32, name="ex")
                row_sum = work.tile([P, 1], F32, name="row_sum")
                nc.scalar.activation(
                    out=ex[:].rearrange("p (c user) -> p c user", c=2),
                    in_=by_row_tile[:, l, :, :],
                    func=ACT.Exp,
                    scale=-1.0,
                    bias=neg_max[:, l : l + 1],
                    accum_out=row_sum[:],
                )
                inv_sum = work.tile([P, 1], F32, name="inv_sum")
                nc.vector.reciprocal(out=inv_sum[:], in_=row_sum[:])
                prob = work.tile([P, USERS], F32, name="prob")
                nc.vector.tensor_scalar(out=prob[:], in0=ex[:], scalar1=inv_sum[:], scalar2=None, op0=ALU.mult)
                nc.sync.dma_start(out=out[(2 * a + l) * P : (2 * a + l + 1) * P, :], in_=prob[:])

        for n in range(WARM_PASSES):
            places = slice(n % PACK * P, (n % PACK + 1) * P)
            nc.tensor.matmul_mx(
                out=y[by_rows[-1]][:, 0:2, :].rearrange("p u n -> p (u n)"),
                lhsT=wq[0][:, places].bitcast(FP8X4),
                lhsT_scale=ws[0][:, places],
                rhs=xq[0][:, 0 : S // 2].bitcast(FP8X4),
                rhs_scale=xs[:, 0 : S // 2],
                start=True,
                stop=True,
            )

        nc.vector.tensor_copy(vq[:], v_table[:].indirect(cand_sb[:]))
        hq_all = keep.tile([P, S], U32, name="hq_all", tag="v_words", align_bytes=64)
        hq = [hq_all[:, c * 2 * P : (c + 1) * 2 * P] for c in range(2)]

        for b in range(S // P - 1):
            hidden(b)
        scores(by_columns[0])
        hidden(S // P - 1)
        for chunk in by_columns[1:]:
            scores(chunk)
        for stage in (weights, totals):
            for chunk in by_columns:
                stage(chunk)
        for chunk in by_rows:
            mix(chunk)
        for a in range(2):
            finish(a)
